import numpy as np
import ml_dtypes


def mxq(x, axis, fmt="e4m3"):
    dtype, down = {"e4m3": (ml_dtypes.float8_e4m3fn, 7), "e5m2": (ml_dtypes.float8_e5m2, 14)}[fmt]
    v = np.moveaxis(np.asarray(x, np.float32).astype(ml_dtypes.bfloat16).astype(np.float64), axis, -1)
    blocks = v.reshape(v.shape[:-1] + (-1, 32))
    amax = np.abs(blocks).max(-1, keepdims=True)
    byte = np.maximum(np.where(amax > 0, np.frexp(amax)[1] - 1 + 127, 0) - down, 1)
    scale = np.exp2(byte - 127.0)
    codes = (blocks / scale).astype(np.float32).astype(dtype).astype(np.float64)
    return np.moveaxis((codes * scale).reshape(v.shape), -1, axis)


WIDE = False


def mx_kscale(k):
    if not WIDE:
        return np.ones(k)
    levels = np.array([10, -10, 5, -5, 0])
    if k % 512:
        return np.exp2(np.random.permutation(np.resize(levels, k // 32))).repeat(32)
    a = np.empty((k // 512, 16))
    for p in range(k // 512):
        a[p, :8] = np.random.permutation(np.resize(levels, 8))
        for g in range(8):
            far = levels[np.abs(levels - a[p, g]) >= 10]
            a[p, g + 8] = far[np.random.randint(len(far))]
    return np.exp2(a.ravel()).repeat(32)


def f64(x):
    return np.asarray(x).astype(np.float64)


def striped(idx):
    return np.tile(np.asarray(idx).reshape(-1, 16).T, (8, 1)).astype(np.uint16)


def unstriped(offs):
    return offs[:16].T.reshape(-1).astype(np.int64)


B, N, T, D, DV, NQ = 2, 512, 2048, 512, 256, 128
PAGE = 64
CAP = 2.0
NEW = 256


def setup_inputs():
    n = np.random.standard_normal
    pages = np.random.permutation(T // PAGE)[:B * N // PAGE]
    idx = (pages[:, None] * PAGE + np.arange(PAGE)[None, :]).reshape(-1)
    s = mx_kscale(D)[:, None]
    u = np.ones(T)
    u[idx] = mx_kscale(B * N)
    r = np.random.uniform(0.5, 2.0, T)
    k = n((D, T)) / s
    v = n((DV, T)) / (u * r)
    new = np.random.permutation(idx.reshape(B, N)[:, -NEW // B:].reshape(-1))
    return {
        "qT": (n((B, D, NQ)) * s * (0.60 / np.sqrt(D))).astype(np.float32),
        "kT": np.where(np.isin(np.arange(T), new)[None, :], n((D, T)), k).astype(np.float32),
        "vT": np.where(np.isin(np.arange(T), new)[None, :], n((DV, T)), v).astype(np.float32),
        "new_kT": k[:, new].astype(np.float32),
        "new_vT": v[:, new].astype(np.float32),
        "vs": np.tile(u * r, (128, 1)).astype(np.float32),
        "offs": striped(idx),
        "slots": striped(new),
    }


def reference(qT, kT, vT, new_kT, new_vT, vs, offs, slots):
    idx = unstriped(offs)
    k = f64(kT)
    k[:, unstriped(slots)] = f64(new_kT)
    v = f64(vT)
    v[:, unstriped(slots)] = f64(new_vT)
    pick = lambda x: x[:, idx].reshape(x.shape[0], B, N).transpose(1, 0, 2)
    q = f64(qT)
    score = mxq(q, 1, "e4m3").transpose(0, 2, 1) @ mxq(pick(k), 1, "e4m3")
    score = CAP * np.tanh(score / CAP)
    m = score.max(-1, keepdims=True)
    p = np.exp(score - m)
    total = p.sum(-1, keepdims=True)
    w = p * pick(f64(vs))[:, :1, :]
    y = mxq(w, 2, "e4m3") @ mxq(pick(v).transpose(0, 2, 1), 1, "e4m3")
    y = y / total
    return y

@@ -1,0 +1,199 @@
+from contextlib import ExitStack
+
+import concourse.mybir as mybir
+from concourse.masks import make_identity
+
+B, N, T, D, DV, NQ, NEW = 2, 512, 2048, 512, 256, 128, 256
+P = 128
+PACK = 4
+FLOPS = 2 * B * NQ * N * (D + DV)
+BYTES = 4 * (B * D * NQ + D * T + DV * T + D * NEW + DV * NEW + T + B * NQ * DV) + 2 * P * (B * N + NEW) // 16
+
+F32 = mybir.dt.float32
+BF16 = mybir.dt.bfloat16
+U32 = mybir.dt.uint32
+U16 = mybir.dt.uint16
+U8 = mybir.dt.uint8
+FP8X4 = mybir.dt.float8_e4m3fn_x4
+ACT = mybir.ActivationFunctionType
+ALU = mybir.AluOpType
+
+PAD = 16
+IL_SPLIT = 336
+
+
+def tile_attend_x_append256_cap_kernel(tc, qT, kT, vT, new_kT, new_vT, vs, offs, slots, out):
+    nc = tc.nc
+    with ExitStack() as ctx:
+        keep = ctx.enter_context(tc.tile_pool(name="keep", bufs=1))
+        psum = ctx.enter_context(tc.psum_pool(name="psum", bufs=1))
+
+        offs_t = keep.tile([P, B * N // 16], U16, name="offs_t")
+        slots_t = keep.tile([P, NEW // 16], U16, name="slots_t")
+        new_k = keep.tile([P, PACK, NEW], F32, name="new_k")
+        new_v = keep.tile([P, 2, NEW], F32, name="new_v")
+        q_raw = keep.tile([P, B, PACK, NQ], F32, name="q_raw")
+        vs_t = keep.tile([P, T], F32, name="vs_t")
+        kp = [keep.tile([P, T], F32, name=f"kp{t}") for t in range(PACK)]
+        vp = [keep.tile([P, T], F32, name=f"vp{h}") for h in range(2)]
+
+        warm = keep.tile([P, 1], F32, name="warm")
+        nc.gpsimd.memset(warm[:], 0.0)
+        nc.scalar.activation(warm[:], warm[:], ACT.Exp)
+        nc.vector.memset(vs_t[:, 0 : T // 2], 0.0)
+        nc.gpsimd.memset(vs_t[:, T // 2 : T], 0.0)
+
+        k_hbm = kT.rearrange("(p j) w -> p j w", j=PACK)
+        nk_hbm = new_kT.rearrange("(p j) w -> p j w", j=PACK)
+        nc.sync.dma_start(offs_t[:], offs)
+        nc.sync.dma_start(slots_t[:], slots)
+        nc.sync.dma_start(new_k[:, 0, :], nk_hbm[:, 0, :])
+        nc.sync.dma_start(vs_t[0:1, :], vs[0:1, :])
+        nc.sync.dma_start(kp[0][:], k_hbm[:, 0, :])
+        nc.sync.dma_start(new_v[:], new_vT.rearrange("(h p) w -> p h w", p=P))
+        nc.sync.dma_start(vp[0][:], vT[0:P, :])
+        nc.sync.dma_start(new_k[:, 1:PACK, :], nk_hbm[:, 1:PACK, :])
+        nc.sync.dma_start(kp[1][:], k_hbm[:, 1, :])
+        nc.sync.dma_start(vp[1][:], vT[P : 2 * P, :])
+        nc.sync.dma_start(kp[2][:], k_hbm[:, 2, :])
+        nc.sync.dma_start(q_raw[:], qT.rearrange("b (p j) w -> p b j w", j=PACK))
+        nc.sync.dma_start(kp[3][:], k_hbm[:, 3, :])
+
+        ident = keep.tile([P, P], F32, name="ident")
+        make_identity(nc, ident[:])
+
+        vsg = keep.tile([P, B * N], F32, name="vsg")
+        nc.vector.tensor_copy(vsg[:], vs_t[:].indirect(offs_t[:]))
+        vsT = []
+        for b in range(B):
+            turned = psum.tile([P, PACK, P], F32, name=f"vs_ps{b}", tag=f"y{b}")
+            for t in range(PACK):
+                nc.tensor.transpose(turned[:, t, :], vsg[:, b * N + t : (b + 1) * N : PACK], ident[:])
+            one = keep.tile([P, PACK], F32, name=f"vsT{b}")
+            nc.scalar.copy(one[:], turned[:, :, 0])
+            vsT.append(one)
+
+        gk = keep.tile([P, 2, B * N, 2], BF16, name="gk", align_bytes=64)
+        gk_words = gk[:].rearrange("p a s j -> p (a s j)").bitcast(F32).rearrange("p (a s) -> p a s", a=2)
+        gv = [keep.tile([P, B, N + PAD], BF16, name=f"gv{h}", align_bytes=64) for h in range(2)]
+
+        def append_k(t):
+            nc.vector.tensor_copy(kp[t][:].indirect(slots_t[:]), new_k[:, t, :])
+
+        def gather_k(t, first, count):
+            nc.vector.tensor_copy(
+                gk[:, t // 2, first : first + count, t % 2],
+                kp[t][:].indirect(offs_t[:, first // 16 : (first + count) // 16]),
+            )
+
+        def append_and_gather_v(h):
+            nc.vector.tensor_copy(vp[h][:].indirect(slots_t[:]), new_v[:, h, :])
+            v16 = keep.tile([P, T], BF16, name=f"v16_{h}")
+            nc.scalar.copy(v16[:], vp[h][:])
+            nc.scalar.activation(gv[h][:, :, 0:N], v16[:].indirect(offs_t[:]), ACT.Copy)
+
+        append_k(0)
+        gather_k(0, 0, B * N)
+        append_and_gather_v(0)
+        append_k(1)
+        gather_k(1, 0, B * N)
+        append_and_gather_v(1)
+        append_k(2)
+        gather_k(2, 0, B * N)
+
+        qx = keep.tile([P, B, NQ, PACK], BF16, name="qx", align_bytes=64)
+        nc.scalar.copy(qx[:], q_raw[:].rearrange("p b j w -> p b w j"))
+
+        append_k(3)
+        for b in range(B):
+            gather_k(3, b * N, N)
+
+        vx = []
+        for b in range(B):
+            turned = psum.tile([P, 2, 2, P], F32, name=f"v_ps{b}")
+            for h in range(2):
+                words = gv[h][:, b, 0:N].bitcast(F32)
+                for u in range(2):
+                    nc.tensor.transpose(turned[:, h, u, :], words[:, u : N // 2 : 2], ident[:])
+            x = keep.tile([P, DV * PACK], BF16, name=f"vx{b}", align_bytes=64)
+            nc.scalar.copy(
+                x[:].bitcast(F32).rearrange("p (h e u) -> p h e u", h=2, u=2),
+                turned[:].rearrange("p h u e -> p h e u"),
+            )
+            vx.append(x)
+
+        qc = keep.tile([P, B * NQ], U32, name="qc", align_bytes=64)
+        qs = keep.tile([P, B * NQ], U8, name="qs", align_bytes=64)
+        nc.vector.quantize_mx(out=qc[:].bitcast(FP8X4), scales=qs[:], in_=qx[:].rearrange("p b w j -> p (b w j)"))
+
+        kx = [keep.tile([P, N * PACK], BF16, name=f"kx{b}", align_bytes=64) for b in range(B)]
+        for b in range(B):
+            kx_words = kx[b][:].bitcast(F32).rearrange("p (s a) -> p s a", a=2)
+            for engine, lo, hi in ((nc.vector.tensor_copy, 0, IL_SPLIT), (nc.scalar.copy, IL_SPLIT, N)):
+                engine(kx_words[:, lo:hi, :], gk_words[:, :, b * N + lo : b * N + hi].rearrange("p a s -> p s a"))
+        scores = []
+        for b in range(B):
+            codes = keep.tile([P, N], U32, name=f"kc{b}", align_bytes=64)
+            scale = keep.tile([P, N], U8, name=f"ksc{b}", align_bytes=64)
+            nc.vector.quantize_mx(out=codes[:].bitcast(FP8X4), scales=scale[:], in_=kx[b][:])
+            acc = psum.tile([P, N], F32, name=f"s_ps{b}")
+            nc.tensor.matmul_mx(
+                out=acc[:],
+                lhsT=qc[:, b * NQ : (b + 1) * NQ].bitcast(FP8X4),
+                lhsT_scale=qs[:, b * NQ : (b + 1) * NQ],
+                rhs=codes[:].bitcast(FP8X4),
+                rhs_scale=scale[:],
+                start=True,
+                stop=True,
+            )
+            scores.append(acc)
+
+        vc, vsc = [], []
+        for b in range(B):
+            codes = keep.tile([P, DV], U32, name=f"vc{b}", align_bytes=64)
+            scale = keep.tile([P, DV], U8, name=f"vsc{b}", align_bytes=64)
+            nc.vector.quantize_mx(out=codes[:].bitcast(FP8X4), scales=scale[:], in_=vx[b][:])
+            vc.append(codes)
+            vsc.append(scale)
+
+        th, prob, total = [], [], []
+        for b in range(B):
+            tanh = keep.tile([P, PACK, P], F32, name=f"th{b}")
+            nc.scalar.activation(tanh[:], scores[b][:].rearrange("q (s t) -> q t s", t=PACK), ACT.Tanh, scale=0.5)
+            minus_m = keep.tile([P, 1], F32, name=f"nm{b}")
+            scaled = keep.tile([P, N], F32, name=f"scaled{b}")
+            nc.vector.tensor_scalar(scaled[:], tanh[:].rearrange("q t s -> q (t s)"), -2.0, None, ALU.mult, ALU.min, accum_out=minus_m[:])
+            p = keep.tile([P, PACK, P], F32, name=f"p{b}")
+            row_sum = keep.tile([P, 1], F32, name=f"l{b}")
+            nc.scalar.activation(p[:], tanh[:], ACT.Exp, bias=minus_m[:], scale=2.0, accum_out=row_sum[:])
+            prob.append(p)
+            total.append(row_sum)
+        for b in range(B):
+            turned = psum.tile([P, PACK, P], F32, name=f"w_ps{b}")
+            for t in range(PACK):
+                nc.tensor.transpose(turned[:, t, :], prob[b][:, t, :], ident[:])
+            wx = keep.tile([P, NQ, PACK], BF16, name=f"wx{b}", align_bytes=64)
+            nc.vector.tensor_tensor(
+                wx[:],
+                turned[:].rearrange("p t q -> p q t"),
+                vsT[b][:].unsqueeze(1).to_broadcast([P, NQ, PACK]),
+                ALU.mult,
+            )
+            codes = keep.tile([P, NQ], U32, name=f"wc{b}", align_bytes=64)
+            scale = keep.tile([P, NQ], U8, name=f"wsc{b}", align_bytes=64)
+            nc.vector.quantize_mx(out=codes[:].bitcast(FP8X4), scales=scale[:], in_=wx[:].rearrange("p q t -> p (q t)"))
+            inv = keep.tile([P, 1], F32, name=f"inv{b}")
+            nc.vector.reciprocal(inv[:], total[b][:])
+            y = psum.tile([P, DV], F32, name=f"y_ps{b}", tag=f"y{b}")
+            nc.tensor.matmul_mx(
+                out=y[:],
+                lhsT=codes[:].bitcast(FP8X4),
+                lhsT_scale=scale[:],
+                rhs=vc[b][:].bitcast(FP8X4),
+                rhs_scale=vsc[b][:],
+                start=True,
+                stop=True,
+            )
+            y_sb = keep.tile([P, DV], F32, name=f"y{b}")
+            nc.scalar.activation(y_sb[:], y[:], ACT.Copy, scale=inv[:])
+            nc.sync.dma_start(out[b], y_sb[:])

@@ -19,7 +19,8 @@ ACT = mybir.ActivationFunctionType
 ALU = mybir.AluOpType
 
 PAD = 16
-IL_SPLIT = 336
+HALF = N // 2
+IL_SHARES = (("vector", 0, 0, HALF), ("scalar", 1, 96, HALF), ("vector", 1, 0, 96))
 
 
 def tile_attend_x_append256_cap_kernel(tc, qT, kT, vT, new_kT, new_vT, vs, offs, slots, out):
@@ -40,16 +41,14 @@ def tile_attend_x_append256_cap_kernel(tc, qT, kT, vT, new_kT, new_vT, vs, offs,
         warm = keep.tile([P, 1], F32, name="warm")
         nc.gpsimd.memset(warm[:], 0.0)
         nc.scalar.activation(warm[:], warm[:], ACT.Exp)
-        nc.vector.memset(vs_t[:, 0 : T // 2], 0.0)
-        nc.gpsimd.memset(vs_t[:, T // 2 : T], 0.0)
-
         k_hbm = kT.rearrange("(p j) w -> p j w", j=PACK)
         nk_hbm = new_kT.rearrange("(p j) w -> p j w", j=PACK)
-        nc.sync.dma_start(offs_t[:], offs)
+        nc.vector.memset(vs_t[:], 0.0)
         nc.sync.dma_start(slots_t[:], slots)
         nc.sync.dma_start(new_k[:, 0, :], nk_hbm[:, 0, :])
-        nc.sync.dma_start(vs_t[0:1, :], vs[0:1, :])
         nc.sync.dma_start(kp[0][:], k_hbm[:, 0, :])
+        nc.sync.dma_start(offs_t[:], offs)
+        nc.sync.dma_start(vs_t[0:1, :], vs[0:1, :])
         nc.sync.dma_start(new_v[:], new_vT.rearrange("(h p) w -> p h w", p=P))
         nc.sync.dma_start(vp[0][:], vT[0:P, :])
         nc.sync.dma_start(new_k[:, 1:PACK, :], nk_hbm[:, 1:PACK, :])
@@ -62,6 +61,23 @@ def tile_attend_x_append256_cap_kernel(tc, qT, kT, vT, new_kT, new_vT, vs, offs,
         ident = keep.tile([P, P], F32, name="ident")
         make_identity(nc, ident[:])
 
+        gk = keep.tile([P, PACK, B, 2, HALF + PAD], BF16, name="gk", align_bytes=64)
+        gv = [keep.tile([P, B, N + PAD], BF16, name=f"gv{h}", align_bytes=64) for h in range(2)]
+
+        def append_k(t):
+            nc.vector.tensor_copy(kp[t][:].indirect(slots_t[:]), new_k[:, t, :])
+
+        def append_and_gather_v(h):
+            nc.vector.tensor_copy(vp[h][:].indirect(slots_t[:]), new_v[:, h, :])
+            v16 = keep.tile([P, T], BF16, name=f"v16_{h}")
+            nc.scalar.copy(v16[:], vp[h][:])
+            nc.scalar.activation(gv[h][:, :, 0:N], v16[:].indirect(offs_t[:]), ACT.Copy)
+
+        append_k(0)
+        k16 = keep.tile([P, T], BF16, name="k16")
+        nc.scalar.copy(k16[:], kp[0][:])
+        nc.scalar.activation(gk[:, 0, :, :, 0:HALF], k16[:].indirect(offs_t[:]), ACT.Copy)
+
         vsg = keep.tile([P, B * N], F32, name="vsg")
         nc.vector.tensor_copy(vsg[:], vs_t[:].indirect(offs_t[:]))
         vsT = []
@@ -73,40 +89,19 @@ def tile_attend_x_append256_cap_kernel(tc, qT, kT, vT, new_kT, new_vT, vs, offs,
             nc.scalar.copy(one[:], turned[:, :, 0])
             vsT.append(one)
 
-        gk = keep.tile([P, 2, B * N, 2], BF16, name="gk", align_bytes=64)
-        gk_words = gk[:].rearrange("p a s j -> p (a s j)").bitcast(F32).rearrange("p (a s) -> p a s", a=2)
-        gv = [keep.tile([P, B, N + PAD], BF16, name=f"gv{h}", align_bytes=64) for h in range(2)]
-
-        def append_k(t):
-            nc.vector.tensor_copy(kp[t][:].indirect(slots_t[:]), new_k[:, t, :])
-
-        def gather_k(t, first, count):
-            nc.vector.tensor_copy(
-                gk[:, t // 2, first : first + count, t % 2],
-                kp[t][:].indirect(offs_t[:, first // 16 : (first + count) // 16]),
-            )
-
-        def append_and_gather_v(h):
-            nc.vector.tensor_copy(vp[h][:].indirect(slots_t[:]), new_v[:, h, :])
-            v16 = keep.tile([P, T], BF16, name=f"v16_{h}")
-            nc.scalar.copy(v16[:], vp[h][:])
-            nc.scalar.activation(gv[h][:, :, 0:N], v16[:].indirect(offs_t[:]), ACT.Copy)
-
-        append_k(0)
-        gather_k(0, 0, B * N)
         append_and_gather_v(0)
         append_k(1)
-        gather_k(1, 0, B * N)
+        nc.vector.tensor_copy(gk[:, 1, :, :, 0:HALF], kp[1][:].indirect(offs_t[:]))
         append_and_gather_v(1)
         append_k(2)
-        gather_k(2, 0, B * N)
+        nc.vector.tensor_copy(gk[:, 2, :, :, 0:HALF], kp[2][:].indirect(offs_t[:]))
 
         qx = keep.tile([P, B, NQ, PACK], BF16, name="qx", align_bytes=64)
         nc.scalar.copy(qx[:], q_raw[:].rearrange("p b j w -> p b w j"))
 
         append_k(3)
         for b in range(B):
-            gather_k(3, b * N, N)
+            nc.vector.tensor_copy(gk[:, 3, b, :, 0:HALF], kp[3][:].indirect(offs_t[:, b * N // 16 : (b + 1) * N // 16]))
 
         vx = []
         for b in range(B):
@@ -128,9 +123,13 @@ def tile_attend_x_append256_cap_kernel(tc, qT, kT, vT, new_kT, new_vT, vs, offs,
 
         kx = [keep.tile([P, N * PACK], BF16, name=f"kx{b}", align_bytes=64) for b in range(B)]
         for b in range(B):
-            kx_words = kx[b][:].bitcast(F32).rearrange("p (s a) -> p s a", a=2)
-            for engine, lo, hi in ((nc.vector.tensor_copy, 0, IL_SPLIT), (nc.scalar.copy, IL_SPLIT, N)):
-                engine(kx_words[:, lo:hi, :], gk_words[:, :, b * N + lo : b * N + hi].rearrange("p a s -> p s a"))
+            kx_cols = kx[b][:].rearrange("p (c i t) -> p c t i", i=4, t=PACK)
+            for engine, half, lo, hi in IL_SHARES:
+                engine = nc.vector.tensor_copy if engine == "vector" else nc.scalar.copy
+                engine(
+                    kx_cols[:, (half * HALF + lo) // 4 : (half * HALF + hi) // 4],
+                    gk[:, :, b, half, lo:hi].rearrange("p t (c i) -> p c t i", i=4),
+                )
         scores = []
         for b in range(B):
             codes = keep.tile([P, N], U32, name=f"kc{b}", align_bytes=64)

@@ -20,7 +20,7 @@ ALU = mybir.AluOpType
 
 PAD = 16
 HALF = N // 2
-IL_SHARES = (("vector", 0, 0, HALF), ("scalar", 1, 96, HALF), ("vector", 1, 0, 96))
+IL_SHARES = (("vector", 0, 0, HALF), ("scalar", 1, 32, HALF), ("vector", 1, 0, 32))
 
 
 def tile_attend_x_append256_cap_kernel(tc, qT, kT, vT, new_kT, new_vT, vs, offs, slots, out):
@@ -49,14 +49,14 @@ def tile_attend_x_append256_cap_kernel(tc, qT, kT, vT, new_kT, new_vT, vs, offs,
         nc.sync.dma_start(kp[0][:], k_hbm[:, 0, :])
         nc.sync.dma_start(offs_t[:], offs)
         nc.sync.dma_start(vs_t[0:1, :], vs[0:1, :])
-        nc.sync.dma_start(new_v[:], new_vT.rearrange("(h p) w -> p h w", p=P))
-        nc.sync.dma_start(vp[0][:], vT[0:P, :])
         nc.sync.dma_start(new_k[:, 1:PACK, :], nk_hbm[:, 1:PACK, :])
         nc.sync.dma_start(kp[1][:], k_hbm[:, 1, :])
-        nc.sync.dma_start(vp[1][:], vT[P : 2 * P, :])
         nc.sync.dma_start(kp[2][:], k_hbm[:, 2, :])
-        nc.sync.dma_start(q_raw[:], qT.rearrange("b (p j) w -> p b j w", j=PACK))
+        nc.sync.dma_start(new_v[:], new_vT.rearrange("(h p) w -> p h w", p=P))
+        nc.sync.dma_start(vp[0][:], vT[0:P, :])
         nc.sync.dma_start(kp[3][:], k_hbm[:, 3, :])
+        nc.sync.dma_start(q_raw[:], qT.rearrange("b (p j) w -> p b j w", j=PACK))
+        nc.sync.dma_start(vp[1][:], vT[P : 2 * P, :])
 
         ident = keep.tile([P, P], F32, name="ident")
         make_identity(nc, ident[:])
@@ -67,16 +67,38 @@ def tile_attend_x_append256_cap_kernel(tc, qT, kT, vT, new_kT, new_vT, vs, offs,
         def append_k(t):
             nc.vector.tensor_copy(kp[t][:].indirect(slots_t[:]), new_k[:, t, :])
 
-        def append_and_gather_v(h):
+        def append_v(h):
             nc.vector.tensor_copy(vp[h][:].indirect(slots_t[:]), new_v[:, h, :])
-            v16 = keep.tile([P, T], BF16, name=f"v16_{h}")
-            nc.scalar.copy(v16[:], vp[h][:])
-            nc.scalar.activation(gv[h][:, :, 0:N], v16[:].indirect(offs_t[:]), ACT.Copy)
+
+        vc, vsc = [], []
+
+        def turn_v(h):
+            turned = psum.tile([P, B, 2, P], F32, name=f"v_ps{h}")
+            for b in range(B):
+                words = gv[h][:, b, 0:N].bitcast(F32)
+                for u in range(2):
+                    nc.tensor.transpose(turned[:, b, u, :], words[:, u : N // 2 : 2], ident[:])
+            x = keep.tile([P, B * P * PACK], BF16, name=f"vx{h}", align_bytes=64)
+            nc.scalar.copy(
+                x[:].bitcast(F32).rearrange("p (b e u) -> p b e u", b=B, u=2),
+                turned[:].rearrange("p b u e -> p b e u"),
+            )
+            return x
+
+        def quantise_v(h, x):
+            codes = keep.tile([P, B * P], U32, name=f"vc{h}", align_bytes=64)
+            scale = keep.tile([P, B * P], U8, name=f"vsc{h}", align_bytes=64)
+            nc.vector.quantize_mx(out=codes[:].bitcast(FP8X4), scales=scale[:], in_=x[:])
+            vc.append(codes)
+            vsc.append(scale)
+
+        def gather_k_scalar(t):
+            k16 = keep.tile([P, T], BF16, name=f"k16_{t}")
+            nc.scalar.copy(k16[:], kp[t][:])
+            nc.scalar.activation(gk[:, t, :, :, 0:HALF], k16[:].indirect(offs_t[:]), ACT.Copy)
 
         append_k(0)
-        k16 = keep.tile([P, T], BF16, name="k16")
-        nc.scalar.copy(k16[:], kp[0][:])
-        nc.scalar.activation(gk[:, 0, :, :, 0:HALF], k16[:].indirect(offs_t[:]), ACT.Copy)
+        gather_k_scalar(0)
 
         vsg = keep.tile([P, B * N], F32, name="vsg")
         nc.vector.tensor_copy(vsg[:], vs_t[:].indirect(offs_t[:]))
@@ -89,37 +111,22 @@ def tile_attend_x_append256_cap_kernel(tc, qT, kT, vT, new_kT, new_vT, vs, offs,
             nc.scalar.copy(one[:], turned[:, :, 0])
             vsT.append(one)
 
-        append_and_gather_v(0)
         append_k(1)
-        nc.vector.tensor_copy(gk[:, 1, :, :, 0:HALF], kp[1][:].indirect(offs_t[:]))
-        append_and_gather_v(1)
+        gather_k_scalar(1)
         append_k(2)
         nc.vector.tensor_copy(gk[:, 2, :, :, 0:HALF], kp[2][:].indirect(offs_t[:]))
 
-        qx = keep.tile([P, B, NQ, PACK], BF16, name="qx", align_bytes=64)
-        nc.scalar.copy(qx[:], q_raw[:].rearrange("p b j w -> p b w j"))
+        append_v(0)
+        v16 = keep.tile([P, T], BF16, name="v16")
+        nc.scalar.copy(v16[:], vp[0][:])
+        nc.scalar.activation(gv[0][:, :, 0:N], v16[:].indirect(offs_t[:]), ACT.Copy)
 
         append_k(3)
         for b in range(B):
             nc.vector.tensor_copy(gk[:, 3, b, :, 0:HALF], kp[3][:].indirect(offs_t[:, b * N // 16 : (b + 1) * N // 16]))
 
-        vx = []
-        for b in range(B):
-            turned = psum.tile([P, 2, 2, P], F32, name=f"v_ps{b}")
-            for h in range(2):
-                words = gv[h][:, b, 0:N].bitcast(F32)
-                for u in range(2):
-                    nc.tensor.transpose(turned[:, h, u, :], words[:, u : N // 2 : 2], ident[:])
-            x = keep.tile([P, DV * PACK], BF16, name=f"vx{b}", align_bytes=64)
-            nc.scalar.copy(
-                x[:].bitcast(F32).rearrange("p (h e u) -> p h e u", h=2, u=2),
-                turned[:].rearrange("p h u e -> p h e u"),
-            )
-            vx.append(x)
-
-        qc = keep.tile([P, B * NQ], U32, name="qc", align_bytes=64)
-        qs = keep.tile([P, B * NQ], U8, name="qs", align_bytes=64)
-        nc.vector.quantize_mx(out=qc[:].bitcast(FP8X4), scales=qs[:], in_=qx[:].rearrange("p b w j -> p (b w j)"))
+        qx = keep.tile([P, B, NQ, PACK], BF16, name="qx", align_bytes=64)
+        nc.gpsimd.tensor_scalar(qx[:], q_raw[:].rearrange("p b j w -> p b w j"), 1.0, 0.0, ALU.mult, ALU.add)
 
         kx = [keep.tile([P, N * PACK], BF16, name=f"kx{b}", align_bytes=64) for b in range(B)]
         for b in range(B):
@@ -130,6 +137,10 @@ def tile_attend_x_append256_cap_kernel(tc, qT, kT, vT, new_kT, new_vT, vs, offs,
                     kx_cols[:, (half * HALF + lo) // 4 : (half * HALF + hi) // 4],
                     gk[:, :, b, half, lo:hi].rearrange("p t (c i) -> p c t i", i=4),
                 )
+        qc = keep.tile([P, B * NQ], U32, name="qc", align_bytes=64)
+        qs = keep.tile([P, B * NQ], U8, name="qs", align_bytes=64)
+        nc.vector.quantize_mx(out=qc[:].bitcast(FP8X4), scales=qs[:], in_=qx[:].rearrange("p b w j -> p (b w j)"))
+
         scores = []
         for b in range(B):
             codes = keep.tile([P, N], U32, name=f"kc{b}", align_bytes=64)
@@ -147,13 +158,9 @@ def tile_attend_x_append256_cap_kernel(tc, qT, kT, vT, new_kT, new_vT, vs, offs,
             )
             scores.append(acc)
 
-        vc, vsc = [], []
-        for b in range(B):
-            codes = keep.tile([P, DV], U32, name=f"vc{b}", align_bytes=64)
-            scale = keep.tile([P, DV], U8, name=f"vsc{b}", align_bytes=64)
-            nc.vector.quantize_mx(out=codes[:].bitcast(FP8X4), scales=scale[:], in_=vx[b][:])
-            vc.append(codes)
-            vsc.append(scale)
+        vx0 = turn_v(0)
+        quantise_v(0, vx0)
+        append_v(1)
 
         th, prob, total = [], [], []
         for b in range(B):
@@ -167,6 +174,9 @@ def tile_attend_x_append256_cap_kernel(tc, qT, kT, vT, new_kT, new_vT, vs, offs,
             nc.scalar.activation(p[:], tanh[:], ACT.Exp, bias=minus_m[:], scale=2.0, accum_out=row_sum[:])
             prob.append(p)
             total.append(row_sum)
+        nc.vector.tensor_copy(gv[1][:, :, 0:N], vp[1][:].indirect(offs_t[:]))
+        vx1 = turn_v(1)
+
         for b in range(B):
             turned = psum.tile([P, PACK, P], F32, name=f"w_ps{b}")
             for t in range(PACK):
@@ -183,16 +193,19 @@ def tile_attend_x_append256_cap_kernel(tc, qT, kT, vT, new_kT, new_vT, vs, offs,
             nc.vector.quantize_mx(out=codes[:].bitcast(FP8X4), scales=scale[:], in_=wx[:].rearrange("p q t -> p (q t)"))
             inv = keep.tile([P, 1], F32, name=f"inv{b}")
             nc.vector.reciprocal(inv[:], total[b][:])
+            if b == 0:
+                quantise_v(1, vx1)
             y = psum.tile([P, DV], F32, name=f"y_ps{b}", tag=f"y{b}")
-            nc.tensor.matmul_mx(
-                out=y[:],
-                lhsT=codes[:].bitcast(FP8X4),
-                lhsT_scale=scale[:],
-                rhs=vc[b][:].bitcast(FP8X4),
-                rhs_scale=vsc[b][:],
-                start=True,
-                stop=True,
-            )
+            for h in range(2):
+                nc.tensor.matmul_mx(
+                    out=y[:, h * P : (h + 1) * P],
+                    lhsT=codes[:].bitcast(FP8X4),
+                    lhsT_scale=scale[:],
+                    rhs=vc[h][:, b * P : (b + 1) * P].bitcast(FP8X4),
+                    rhs_scale=vsc[h][:, b * P : (b + 1) * P],
+                    start=True,
+                    stop=True,
+                )
             y_sb = keep.tile([P, DV], F32, name=f"y{b}")
             nc.scalar.activation(y_sb[:], y[:], ACT.Copy, scale=inv[:])
             nc.sync.dma_start(out[b], y_sb[:])

from contextlib import ExitStack

import concourse.mybir as mybir
from concourse.masks import make_identity

B, N, T, D, DV, NQ, NEW = 2, 512, 2048, 512, 256, 128, 256
P = 128
PACK = 4
FLOPS = 2 * B * NQ * N * (D + DV)
BYTES = 4 * (B * D * NQ + D * T + DV * T + D * NEW + DV * NEW + T + B * NQ * DV) + 2 * P * (B * N + NEW) // 16

F32 = mybir.dt.float32
BF16 = mybir.dt.bfloat16
U32 = mybir.dt.uint32
U16 = mybir.dt.uint16
U8 = mybir.dt.uint8
FP8X4 = mybir.dt.float8_e4m3fn_x4
ACT = mybir.ActivationFunctionType
ALU = mybir.AluOpType

PAD = 16
HALF = N // 2
IL_SHARES = (("vector", 0, 0, HALF), ("scalar", 1, 32, HALF), ("vector", 1, 0, 32))


def tile_attend_x_append256_cap_kernel(tc, qT, kT, vT, new_kT, new_vT, vs, offs, slots, out):
    nc = tc.nc
    with ExitStack() as ctx:
        keep = ctx.enter_context(tc.tile_pool(name="keep", bufs=1))
        psum = ctx.enter_context(tc.psum_pool(name="psum", bufs=1))

        offs_t = keep.tile([P, B * N // 16], U16, name="offs_t")
        slots_t = keep.tile([P, NEW // 16], U16, name="slots_t")
        new_k = keep.tile([P, PACK, NEW], F32, name="new_k")
        new_v = keep.tile([P, 2, NEW], F32, name="new_v")
        q_raw = keep.tile([P, B, PACK, NQ], F32, name="q_raw")
        vs_t = keep.tile([P, T], F32, name="vs_t")
        kp = [keep.tile([P, T], F32, name=f"kp{t}") for t in range(PACK)]
        vp = [keep.tile([P, T], F32, name=f"vp{h}") for h in range(2)]

        warm = keep.tile([P, 1], F32, name="warm")
        nc.gpsimd.memset(warm[:], 0.0)
        nc.scalar.activation(warm[:], warm[:], ACT.Exp)
        k_hbm = kT.rearrange("(p j) w -> p j w", j=PACK)
        nk_hbm = new_kT.rearrange("(p j) w -> p j w", j=PACK)
        nc.vector.memset(vs_t[:], 0.0)
        nc.sync.dma_start(slots_t[:], slots)
        nc.sync.dma_start(new_k[:, 0, :], nk_hbm[:, 0, :])
        nc.sync.dma_start(kp[0][:], k_hbm[:, 0, :])
        nc.sync.dma_start(offs_t[:], offs)
        nc.sync.dma_start(vs_t[0:1, :], vs[0:1, :])
        nc.sync.dma_start(new_k[:, 1:PACK, :], nk_hbm[:, 1:PACK, :])
        nc.sync.dma_start(kp[1][:], k_hbm[:, 1, :])
        nc.sync.dma_start(kp[2][:], k_hbm[:, 2, :])
        nc.sync.dma_start(new_v[:], new_vT.rearrange("(h p) w -> p h w", p=P))
        nc.sync.dma_start(vp[0][:], vT[0:P, :])
        nc.sync.dma_start(kp[3][:], k_hbm[:, 3, :])
        nc.sync.dma_start(q_raw[:], qT.rearrange("b (p j) w -> p b j w", j=PACK))
        nc.sync.dma_start(vp[1][:], vT[P : 2 * P, :])

        ident = keep.tile([P, P], F32, name="ident")
        make_identity(nc, ident[:])

        gk = keep.tile([P, PACK, B, 2, HALF + PAD], BF16, name="gk", align_bytes=64)
        gv = [keep.tile([P, B, N + PAD], BF16, name=f"gv{h}", align_bytes=64) for h in range(2)]

        def append_k(t):
            nc.vector.tensor_copy(kp[t][:].indirect(slots_t[:]), new_k[:, t, :])

        def append_v(h):
            nc.vector.tensor_copy(vp[h][:].indirect(slots_t[:]), new_v[:, h, :])

        vc, vsc = [], []

        def turn_v(h):
            turned = psum.tile([P, B, 2, P], F32, name=f"v_ps{h}")
            for b in range(B):
                words = gv[h][:, b, 0:N].bitcast(F32)
                for u in range(2):
                    nc.tensor.transpose(turned[:, b, u, :], words[:, u : N // 2 : 2], ident[:])
            x = keep.tile([P, B * P * PACK], BF16, name=f"vx{h}", align_bytes=64)
            nc.scalar.copy(
                x[:].bitcast(F32).rearrange("p (b e u) -> p b e u", b=B, u=2),
                turned[:].rearrange("p b u e -> p b e u"),
            )
            return x

        def quantise_v(h, x):
            codes = keep.tile([P, B * P], U32, name=f"vc{h}", align_bytes=64)
            scale = keep.tile([P, B * P], U8, name=f"vsc{h}", align_bytes=64)
            nc.vector.quantize_mx(out=codes[:].bitcast(FP8X4), scales=scale[:], in_=x[:])
            vc.append(codes)
            vsc.append(scale)

        def gather_k_scalar(t):
            k16 = keep.tile([P, T], BF16, name=f"k16_{t}")
            nc.scalar.copy(k16[:], kp[t][:])
            nc.scalar.activation(gk[:, t, :, :, 0:HALF], k16[:].indirect(offs_t[:]), ACT.Copy)

        append_k(0)
        gather_k_scalar(0)

        vsg = keep.tile([P, B * N], F32, name="vsg")
        nc.vector.tensor_copy(vsg[:], vs_t[:].indirect(offs_t[:]))
        vsT = []
        for b in range(B):
            turned = psum.tile([P, PACK, P], F32, name=f"vs_ps{b}", tag=f"y{b}")
            for t in range(PACK):
                nc.tensor.transpose(turned[:, t, :], vsg[:, b * N + t : (b + 1) * N : PACK], ident[:])
            one = keep.tile([P, PACK], F32, name=f"vsT{b}")
            nc.scalar.copy(one[:], turned[:, :, 0])
            vsT.append(one)

        append_k(1)
        gather_k_scalar(1)
        append_k(2)
        nc.vector.tensor_copy(gk[:, 2, :, :, 0:HALF], kp[2][:].indirect(offs_t[:]))

        append_v(0)
        v16 = keep.tile([P, T], BF16, name="v16")
        nc.scalar.copy(v16[:], vp[0][:])
        nc.scalar.activation(gv[0][:, :, 0:N], v16[:].indirect(offs_t[:]), ACT.Copy)

        append_k(3)
        for b in range(B):
            nc.vector.tensor_copy(gk[:, 3, b, :, 0:HALF], kp[3][:].indirect(offs_t[:, b * N // 16 : (b + 1) * N // 16]))

        qx = keep.tile([P, B, NQ, PACK], BF16, name="qx", align_bytes=64)
        nc.gpsimd.tensor_scalar(qx[:], q_raw[:].rearrange("p b j w -> p b w j"), 1.0, 0.0, ALU.mult, ALU.add)

        kx = [keep.tile([P, N * PACK], BF16, name=f"kx{b}", align_bytes=64) for b in range(B)]
        for b in range(B):
            kx_cols = kx[b][:].rearrange("p (c i t) -> p c t i", i=4, t=PACK)
            for engine, half, lo, hi in IL_SHARES:
                engine = nc.vector.tensor_copy if engine == "vector" else nc.scalar.copy
                engine(
                    kx_cols[:, (half * HALF + lo) // 4 : (half * HALF + hi) // 4],
                    gk[:, :, b, half, lo:hi].rearrange("p t (c i) -> p c t i", i=4),
                )
        qc = keep.tile([P, B * NQ], U32, name="qc", align_bytes=64)
        qs = keep.tile([P, B * NQ], U8, name="qs", align_bytes=64)
        nc.vector.quantize_mx(out=qc[:].bitcast(FP8X4), scales=qs[:], in_=qx[:].rearrange("p b w j -> p (b w j)"))

        scores = []
        for b in range(B):
            codes = keep.tile([P, N], U32, name=f"kc{b}", align_bytes=64)
            scale = keep.tile([P, N], U8, name=f"ksc{b}", align_bytes=64)
            nc.vector.quantize_mx(out=codes[:].bitcast(FP8X4), scales=scale[:], in_=kx[b][:])
            acc = psum.tile([P, N], F32, name=f"s_ps{b}")
            nc.tensor.matmul_mx(
                out=acc[:],
                lhsT=qc[:, b * NQ : (b + 1) * NQ].bitcast(FP8X4),
                lhsT_scale=qs[:, b * NQ : (b + 1) * NQ],
                rhs=codes[:].bitcast(FP8X4),
                rhs_scale=scale[:],
                start=True,
                stop=True,
            )
            scores.append(acc)

        vx0 = turn_v(0)
        quantise_v(0, vx0)
        append_v(1)

        th, prob, total = [], [], []
        for b in range(B):
            tanh = keep.tile([P, PACK, P], F32, name=f"th{b}")
            nc.scalar.activation(tanh[:], scores[b][:].rearrange("q (s t) -> q t s", t=PACK), ACT.Tanh, scale=0.5)
            minus_m = keep.tile([P, 1], F32, name=f"nm{b}")
            scaled = keep.tile([P, N], F32, name=f"scaled{b}")
            nc.vector.tensor_scalar(scaled[:], tanh[:].rearrange("q t s -> q (t s)"), -2.0, None, ALU.mult, ALU.min, accum_out=minus_m[:])
            p = keep.tile([P, PACK, P], F32, name=f"p{b}")
            row_sum = keep.tile([P, 1], F32, name=f"l{b}")
            nc.scalar.activation(p[:], tanh[:], ACT.Exp, bias=minus_m[:], scale=2.0, accum_out=row_sum[:])
            prob.append(p)
            total.append(row_sum)
        nc.vector.tensor_copy(gv[1][:, :, 0:N], vp[1][:].indirect(offs_t[:]))
        vx1 = turn_v(1)

        for b in range(B):
            turned = psum.tile([P, PACK, P], F32, name=f"w_ps{b}")
            for t in range(PACK):
                nc.tensor.transpose(turned[:, t, :], prob[b][:, t, :], ident[:])
            wx = keep.tile([P, NQ, PACK], BF16, name=f"wx{b}", align_bytes=64)
            nc.vector.tensor_tensor(
                wx[:],
                turned[:].rearrange("p t q -> p q t"),
                vsT[b][:].unsqueeze(1).to_broadcast([P, NQ, PACK]),
                ALU.mult,
            )
            codes = keep.tile([P, NQ], U32, name=f"wc{b}", align_bytes=64)
            scale = keep.tile([P, NQ], U8, name=f"wsc{b}", align_bytes=64)
            nc.vector.quantize_mx(out=codes[:].bitcast(FP8X4), scales=scale[:], in_=wx[:].rearrange("p q t -> p (q t)"))
            inv = keep.tile([P, 1], F32, name=f"inv{b}")
            nc.vector.reciprocal(inv[:], total[b][:])
            if b == 0:
                quantise_v(1, vx1)
            y = psum.tile([P, DV], F32, name=f"y_ps{b}", tag=f"y{b}")
            for h in range(2):
                nc.tensor.matmul_mx(
                    out=y[:, h * P : (h + 1) * P],
                    lhsT=codes[:].bitcast(FP8X4),
                    lhsT_scale=scale[:],
                    rhs=vc[h][:, b * P : (b + 1) * P].bitcast(FP8X4),
                    rhs_scale=vsc[h][:, b * P : (b + 1) * P],
                    start=True,
                    stop=True,
                )
            y_sb = keep.tile([P, DV], F32, name=f"y{b}")
            nc.scalar.activation(y_sb[:], y[:], ACT.Copy, scale=inv[:])
            nc.sync.dma_start(out[b], y_sb[:])
